import numpy as np
import ml_dtypes


def mxq(x, axis, fmt="e4m3"):
    dtype, down = {"e4m3": (ml_dtypes.float8_e4m3fn, 7), "e5m2": (ml_dtypes.float8_e5m2, 14)}[fmt]
    v = np.moveaxis(np.asarray(x, np.float32).astype(ml_dtypes.bfloat16).astype(np.float64), axis, -1)
    blocks = v.reshape(v.shape[:-1] + (-1, 32))
    amax = np.abs(blocks).max(-1, keepdims=True)
    byte = np.maximum(np.where(amax > 0, np.frexp(amax)[1] - 1 + 127, 0) - down, 1)
    scale = np.exp2(byte - 127.0)
    codes = (blocks / scale).astype(np.float32).astype(dtype).astype(np.float64)
    return np.moveaxis((codes * scale).reshape(v.shape), -1, axis)


WIDE = False


def mx_kscale(k):
    if not WIDE:
        return np.ones(k)
    levels = np.array([10, -10, 5, -5, 0])
    if k % 512:
        return np.exp2(np.random.permutation(np.resize(levels, k // 32))).repeat(32)
    a = np.empty((k // 512, 16))
    for p in range(k // 512):
        a[p, :8] = np.random.permutation(np.resize(levels, 8))
        for g in range(8):
            far = levels[np.abs(levels - a[p, g]) >= 10]
            a[p, g + 8] = far[np.random.randint(len(far))]
    return np.exp2(a.ravel()).repeat(32)


BF16 = ml_dtypes.bfloat16


def bf(x):
    return np.asarray(x, np.float32).astype(BF16)


def f64(x):
    return np.asarray(x).astype(np.float64)


E2M1 = np.array([0.0, 0.5, 1.0, 1.5, 2.0, 3.0, 4.0, 6.0, -0.0, -0.5, -1.0, -1.5, -2.0, -3.0, -4.0, -6.0])


def pack_weight(w, fmt):
    k, n = w.shape
    w = f64(bf(w)).reshape(k // 32, 32, n)
    amax = np.abs(w).max(1)
    if fmt == "e4m3":
        byte = np.frexp(amax)[1] - 1 + 127 - 7
    else:
        mant, ex = np.frexp(amax / 6.0)
        byte = np.where(mant > 0.5, ex, ex - 1) + 127
    byte = np.clip(np.where(amax > 0, byte, 1), 1, 254)
    scaled = (w * np.exp2(127.0 - byte)[:, None, :]).reshape(k, n).astype(np.float32)
    by_word = np.ascontiguousarray(scaled.reshape(k // 512, 128, 4, n).transpose(0, 1, 3, 2))
    if fmt == "e4m3":
        words = by_word.astype(ml_dtypes.float8_e4m3fn).view(np.uint8)
    else:
        c = by_word.astype(ml_dtypes.float4_e2m1fn).view(np.uint8) & 0xF
        words = c[..., 0::2] | (c[..., 1::2] << 4)
    return np.ascontiguousarray(words), np.ascontiguousarray(byte.astype(np.uint8).reshape(k // 512, 16, n))


def unpack_weight(words, scales, fmt):
    g, p, n, _ = words.shape
    if fmt == "e4m3":
        vals = np.ascontiguousarray(words).view(ml_dtypes.float8_e4m3fn).astype(np.float64)
    else:
        nib = np.empty((g, p, n, 4), np.uint8)
        nib[..., 0::2] = words & 0xF
        nib[..., 1::2] = words >> 4
        vals = E2M1[nib]
    vals = vals * np.repeat(np.exp2(scales.astype(np.float64) - 127.0), 8, axis=1)[..., None]
    return vals.transpose(0, 1, 3, 2).reshape(g * 512, n)
def pack4(w):
    words, scales = pack_weight(w, "e2m1")
    return words.reshape(words.shape[0], 128, -1), scales


def unpack4(words, scales):
    return unpack_weight(words.reshape(words.shape[0], 128, -1, 2), scales, "e2m1")


def planes(Y):
    n, m = Y.shape
    b = f64(bf(Y)).reshape(n // 32, 32, m)
    amax = np.abs(b).max(1)
    byte = np.clip(np.where(amax > 0, np.frexp(amax)[1] - 1 + 127 - 7, 1), 1, 254)
    codes = (b * np.exp2(127.0 - byte)[:, None, :]).reshape(n, m).astype(np.float32).astype(ml_dtypes.float8_e4m3fn).view(np.uint8)
    words = codes.reshape(n // 512, 128, 4, m).transpose(0, 1, 3, 2)
    return np.ascontiguousarray(words), np.ascontiguousarray(byte.astype(np.uint8).reshape(n // 512, 16, m))


R, T1, T2, NU, D = 1024, 1024, 1536, 512, 1024
FILTER_GAIN = 0.7
PRECODER_GAIN = 0.7
POWER_SPREAD = 0.7

def setup_inputs():
    s1 = mx_kscale(T1)
    s2 = mx_kscale(T2)
    t = mx_kscale(R)
    H1 = bf(np.random.randn(R, T1) * t[:, None] * s1[None, :])
    H2 = bf(np.random.randn(R, T2) * t[:, None] * s2[None, :])
    V1 = bf(PRECODER_GAIN / np.sqrt(T1) * np.random.randn(T1, D) / s1[:, None])
    V2_words, V2_scales = pack4(PRECODER_GAIN / np.sqrt(T2) * np.random.randn(T2, D) / s2[:, None])
    U1 = bf(FILTER_GAIN / np.sqrt(R) * np.random.randn(R, NU) / t[:, None])
    U2 = bf(FILTER_GAIN / np.sqrt(R) * np.random.randn(R, NU) / t[:, None])
    power = bf(np.exp(POWER_SPREAD * np.random.randn(D)))
    return {"H1": H1, "V1": V1, "H2": H2, "V2_words": V2_words, "V2_scales": V2_scales,
            "U1": U1, "U2": U2, "power": power}

def reference(H1, V1, H2, V2_words, V2_scales, U1, U2, power):
    G = ((mxq(f64(H1), 1, "e4m3") @ mxq(f64(V1), 0, "e4m3"))
         + (mxq(f64(H2), 1, "e4m3") @ unpack4(V2_words, V2_scales)))
    Gq = mxq(G, 0, "e4m3")
    F1 = mxq(f64(U1), 0, "e4m3").T @ Gq
    F2 = mxq(f64(U2), 0, "e4m3").T @ Gq
    y = (F1 ** 2 + F2 ** 2) * f64(power)[None, :]
    Y = y.T
    words, scales = planes(Y)
    return y, words, scales

@@ -1,0 +1,489 @@
+from contextlib import ExitStack
+
+import concourse.mybir as mybir
+from concourse.masks import make_identity
+
+R, T1, T2, NU, D = 1024, 1024, 1536, 512, 1024
+FLOPS = 2 * R * (T1 + T2) * D + 2 * 2 * NU * R * D
+
+F32 = mybir.dt.float32
+BF16 = mybir.dt.bfloat16
+I32 = mybir.dt.int32
+U32 = mybir.dt.uint32
+U8 = mybir.dt.uint8
+FP8X4 = mybir.dt.float8_e4m3fn_x4
+FP4X4 = mybir.dt.float4_e2m1fn_x4
+ADD = mybir.AluOpType.add
+MULT = mybir.AluOpType.mult
+SQUARE = mybir.ActivationFunctionType.Square
+
+P = 128
+PACK = 4
+KP = P * PACK
+BANK = 512
+CH = 128
+NCH = D // CH
+ROW_TILES = R // P
+EARLY = 4
+
+
+def tile_joint_precoding_interference_leakage_k6_kernel(
+    tc, H1, V1, H2, V2_words, V2_scales, U1, U2, power, out_0, out_1, out_2
+):
+    nc = tc.nc
+    with ExitStack() as ctx:
+        keep = ctx.enter_context(tc.tile_pool(name="keep", bufs=1))
+        stage = ctx.enter_context(tc.tile_pool(name="stage", bufs=3))
+        psum = ctx.enter_context(tc.psum_pool(name="psum", bufs=1))
+        ctx.enter_context(tc.manual_schedule())
+
+        counter = []
+
+        def fresh(prefix):
+            counter.append(0)
+            return "%s%d" % (prefix, len(counter))
+
+        def bank(k):
+            return psum.tile([P, BANK], F32, name=fresh("ps"), tag="bank%d" % k)
+
+        turns = {}
+
+        def rotate(role, banks):
+            n = turns.get(role, 0)
+            turns.update({role: n + 1})
+            return bank(banks[n % len(banks)])
+
+        def planes(name, width):
+            codes = keep.tile([P, width], U32, name=name + "c", align_bytes=64)
+            scales = keep.tile([P, width], U8, name=name + "s", align_bytes=64)
+            return codes, scales
+
+        def quantize(pair, cols, src):
+            nc.vector.quantize_mx(out=pair[0][:, cols].bitcast(FP8X4), scales=pair[1][:, cols], in_=src)
+
+        h_rows = {1: H1.rearrange("(g m t) k -> g t m k", g=2, t=PACK), 2: H2.rearrange("(g m t) k -> g t m k", g=2, t=PACK)}
+        h_raw = {}
+
+        def load_h(which, i):
+            width = T1 if which == 1 else T2
+            raw = keep.tile([P, width], BF16, name="h%d_%d" % (which, i))
+            nc.sync.dma_start(out=raw[:], in_=h_rows[which][i // PACK, i % PACK])
+            h_raw[which, i] = raw
+
+        v2_words = {}
+
+        def load_v2(half):
+            words = keep.tile([P, 3, D], U8, name="v2w%d" % half, align_bytes=64)
+            src = V2_words.rearrange("g p n -> p g n")[:, :, half * D : (half + 1) * D]
+            nc.sync.dma_start(out=words[:].bitcast(I32), in_=src.bitcast(I32))
+            v2_words[half] = words
+
+        v2_scale = {}
+
+        def load_v2_scales(half, engine):
+            plane = keep.tile([P, 3, BANK], U8, name="v2s%d" % half, align_bytes=64)
+            nc.vector.memset(plane[:].bitcast(I32), 0)
+            rows = V2_scales.rearrange("g q n -> q g n")[:, :, half * BANK : (half + 1) * BANK]
+            for quad in range(4):
+                engine.dma_start(
+                    out=plane[32 * quad : 32 * quad + 4].bitcast(I32), in_=rows[4 * quad : 4 * quad + 4].bitcast(I32)
+                )
+            v2_scale[half] = plane
+
+        raw_of = {}
+
+        def load_kfirst(key, src, c, col0, width):
+            raw = keep.tile([P, PACK, width], BF16, name="raw%s_%d_%d" % (key, c, col0))
+            nc.sync.dma_start(
+                out=raw[:], in_=src[c * KP : (c + 1) * KP, col0 : col0 + width].rearrange("(p j) n -> p j n", j=PACK)
+            )
+            for x in range(col0, col0 + width, 256):
+                raw_of[key, c, x // 256] = raw[:, :, x - col0 : x - col0 + 256]
+
+        kq = {}
+        grouped_of = {}
+
+        def interleave(piece, engine):
+            grouped = stage.tile([P, 256 * PACK], BF16, name=fresh("grp"), tag="grp" + engine, bufs=4, align_bytes=64)
+            dst = grouped[:].rearrange("p (c i t) -> p c t i", i=4, t=PACK)
+            src = raw_of[piece].rearrange("p t (c i) -> p c t i", i=4)
+            if engine == "V":
+                nc.vector.tensor_copy(out=dst, in_=src)
+            else:
+                nc.scalar.copy(out=dst, in_=src)
+            grouped_of[piece] = grouped
+
+        def quantize_piece(piece):
+            key, c, x = piece
+            if (key, c, x // 2) not in kq:
+                kq[key, c, x // 2] = planes("kq%s_%d_%d" % piece, 512)
+            quantize(kq[key, c, x // 2], slice((x % 2) * 256, (x % 2 + 1) * 256), grouped_of[piece][:])
+
+        ident = keep.tile([P, P], F32, name="ident")
+        PARTS = ((2, 0, 2), (2, 2, 1), (1, 0, 2))
+        h_turned = {}
+        hq = {}
+
+        def turn_h(i, part):
+            which, c0, n = PARTS[part]
+            words = h_raw[which, i][:].bitcast(F32)
+            ps = rotate("T", (3, 4, 5, 6, 7))
+            for c in range(n):
+                for u in range(2):
+                    w0 = 256 * (c0 + c)
+                    slot = 2 * c + u
+                    nc.tensor.transpose(ps[:, slot * P : (slot + 1) * P], words[:, w0 + u : w0 + 256 : 2], ident[:])
+            turned = stage.tile([P, 1024], BF16, name=fresh("ht"), tag="ht", bufs=4, align_bytes=64)
+            nc.scalar.copy(
+                out=turned[:, : n * KP].bitcast(F32).rearrange("p (c r u) -> p c r u", c=n, u=2),
+                in_=ps[:, : n * 256].rearrange("p (c u r) -> p c r u", c=n, u=2),
+            )
+            h_turned[i, part] = turned
+
+        def quantize_h(i, part):
+            n = PARTS[part][2]
+            hq[i, part] = planes("hq%d_%d" % (i, part), n * P)
+            quantize(hq[i, part], slice(0, n * P), h_turned[i, part][:, : n * KP])
+
+        g_bank = {}
+
+        def g_passes(i, out, d0, w, first, last):
+            half, x0 = divmod(d0, BANK)
+            for c in range(first, last):
+                if c < 3:
+                    pair, off = hq[i, c // 2], (c % 2) * P
+                    rhs = v2_words[half][:, c, 2 * x0 : 2 * (x0 + w)].bitcast(FP4X4)
+                    rhs_scale = v2_scale[half][:, c, x0 : x0 + w]
+                else:
+                    pair, off = hq[i, 2], (c - 3) * P
+                    mov = kq["v", c - 3, half]
+                    rhs = mov[0][:, x0 : x0 + w].bitcast(FP8X4)
+                    rhs_scale = mov[1][:, x0 : x0 + w]
+                nc.tensor.matmul_mx(
+                    out=out,
+                    lhsT=pair[0][:, off : off + P].bitcast(FP8X4),
+                    lhsT_scale=pair[1][:, off : off + P],
+                    rhs=rhs,
+                    rhs_scale=rhs_scale,
+                    start=(c == 0),
+                    stop=(c == 4),
+                )
+
+        wide_bank = {}
+        wide_bf = {}
+
+        def wide_passes(i, half, first, last):
+            if first == 0:
+                wide_bank[i, half] = rotate("W", (0, 1, 2)) if half == 0 else next_bank()
+            g_passes(i, wide_bank[i, half][:], half * BANK, BANK, first, last)
+
+        def empty_wide(i, half):
+            g, t = divmod(i, PACK)
+            if t == 0:
+                wide_bf[g, half] = stage.tile([P, PACK, BANK], BF16, name=fresh("gw"), tag="gw", bufs=2)
+                for x in range(2):
+                    raw_of["g", g, 2 * half + x] = wide_bf[g, half][:, :, 256 * x : 256 * (x + 1)]
+            nc.scalar.copy(out=wide_bf[g, half][:, t, :], in_=wide_bank[i, half][:])
+
+        g_bf = {}
+        gq = {}
+
+        def empty_g(g, j, engine="S"):
+            dst = stage.tile([P, CH * PACK], BF16, name=fresh("gb"), tag="gb", bufs=5, align_bytes=64)
+            o = dst[:].rearrange("p (d t) -> p d t", t=PACK)
+            s = g_bank[g, j][:].rearrange("p (t d) -> p d t", t=PACK)
+            if engine == "V":
+                nc.vector.tensor_copy(out=o, in_=s)
+            else:
+                nc.scalar.copy(out=o, in_=s)
+            g_bf[g, j] = dst
+
+        def quantize_g(g, j):
+            if j % 4 == 0:
+                kq["g", g, j // 4] = planes("gq%d_%d" % (g, j // 4), BANK)
+            quantize(kq["g", g, j // 4], slice((j % 4) * CH, (j % 4 + 1) * CH), g_bf[g, j][:])
+
+        pw = keep.tile([P, D], BF16, name="pw")
+        order = [2, 3, 4, 0, 5, 6, 7, 1]
+        taken = []
+
+        def next_bank():
+            taken.append(0)
+            return bank(order[(len(taken) - 1) % 8])
+
+        sq_of = {}
+        y_of = {}
+
+        def f_pass(ps, o, j0, w, a, f, g):
+            st = kq["u%d" % (f + 1), g, 0]
+            mov = kq["g", g, j0 // 4]
+            cols = slice((j0 % 4) * CH, (j0 % 4) * CH + w)
+            nc.tensor.matmul_mx(
+                out=ps[:, o : o + w],
+                lhsT=st[0][:, a * P : (a + 1) * P].bitcast(FP8X4),
+                lhsT_scale=st[1][:, a * P : (a + 1) * P],
+                rhs=mov[0][:, cols].bitcast(FP8X4),
+                rhs_scale=mov[1][:, cols],
+                start=(g == 0),
+                stop=(g == 1),
+            )
+
+        def square(ps, key, width):
+            sq = stage.tile([P, BANK], F32, name=fresh("sq"), tag="sq", bufs=4)
+            nc.scalar.activation(out=sq[:, :width], in_=ps[:, :width], func=SQUARE)
+            sq_of[key] = sq[:, :width]
+
+        def f_passes(j0, nj, b):
+            w = nj * CH
+            per = 2 // nj
+            ps = next_bank()
+            for al in range(per):
+                for f in range(2):
+                    for g in range(2):
+                        f_pass(ps, (2 * al + f) * w, j0, w, b * per + al, f, g)
+            square(ps, (j0, b), BANK)
+
+        sum_of = {}
+
+        def add_squares(j0, nj, b, per):
+            w = nj * CH
+            v = sq_of[j0, b].rearrange("p (a f w) -> p a f w", f=2, w=w)
+            s = stage.tile([P, per, w], F32, name=fresh("sum"), tag="sum", bufs=4)
+            nc.vector.tensor_tensor(out=s[:], in0=v[:, :, 0, :], in1=v[:, :, 1, :], op=ADD)
+            sum_of[j0, b] = s
+
+        def weigh(j0, nj, b, per):
+            w = nj * CH
+            if b == 0:
+                y_of[j0] = stage.tile([P, 4, w], F32, name=fresh("y"), tag="y", bufs=3)
+            gain = pw[:, j0 * CH : j0 * CH + w].unsqueeze(1).to_broadcast([P, per, w])
+            nc.vector.tensor_tensor(out=y_of[j0][:, b * per : (b + 1) * per, :], in0=sum_of[j0, b][:], in1=gain, op=MULT)
+
+        def store_y(j0, nj):
+            dst = out_0[:, j0 * CH : (j0 + nj) * CH].rearrange("(a u) d -> u a d", u=P)
+            nc.sync.dma_start(out=dst, in_=y_of[j0][:])
+
+        y_bf = {}
+
+        def round_y(j0, jj, engine="V"):
+            dst = stage.tile([P, 4 * CH], BF16, name=fresh("yb"), tag="yb", bufs=8)
+            (nc.vector.tensor_copy if engine == "V" else nc.scalar.copy)(
+                out=dst[:].rearrange("p (u a q e) -> p u a q e", u=2, a=4, e=2),
+                in_=y_of[j0][:, :, jj * CH : (jj + 1) * CH].rearrange("p a (q u e) -> p u a q e", u=2, e=2),
+            )
+            y_bf[j0 + jj] = dst
+
+        y_turned = {}
+
+        def turn_y(js, step=1):
+            ps = next_bank()
+            n = len(js)
+            for x, j in enumerate(js):
+                words = y_bf[j][:].bitcast(F32)
+                for u in range(2):
+                    slot = 2 * x + u
+                    nc.tensor.transpose(ps[:, slot * P : (slot + 1) * P], words[:, u * P : (u + 1) * P] if step == 1 else words[:, u::2], ident[:])
+            turned = stage.tile([P, 1024], BF16, name=fresh("yt"), tag="ht", bufs=4, align_bytes=64)
+            nc.scalar.copy(
+                out=turned[:, : n * KP].bitcast(F32).rearrange("p (c r u) -> p c r u", c=n, u=2),
+                in_=ps[:, : n * 256].rearrange("p (c u r) -> p c r u", c=n, u=2),
+            )
+            for x, j in enumerate(js):
+                y_turned[j] = turned[:, x * KP : (x + 1) * KP]
+
+        y_codes = [keep.tile([P, 4 * P], U32, name="yc%d" % g, align_bytes=64) for g in range(2)]
+        y_scales = [keep.tile([P, P], U8, name="ys%d" % g, align_bytes=64) for g in range(2)]
+
+        def quantize_y(j):
+            g, jj = divmod(j, 4)
+            nc.vector.quantize_mx(
+                out=y_codes[g][:, jj * P : (jj + 1) * P].bitcast(FP8X4), scales=y_scales[g][4 * jj :, :], in_=y_turned[j]
+            )
+
+        def store_codes(g, first, last, engines):
+            dst = out_1[g].rearrange("(j q) (a m) t -> a q j (m t)", j=4, a=4)
+            for a in range(4):
+                src = y_codes[g][32 * a : 32 * a + 32, first * P : last * P].rearrange("q (j m) -> q j m", m=P)
+                engines[a % len(engines)].dma_start(out=dst[a, :, first:last, :].bitcast(I32), in_=src.bitcast(I32))
+
+        def store_scales(g, engines):
+            for a in range(4):
+                engines[a % len(engines)].dma_start(
+                    out=out_2[g, :, a * P : (a + 1) * P].bitcast(I32), in_=y_scales[g][32 * a : 32 * a + 16, :].bitcast(I32)
+                )
+
+        make_identity(nc, ident[:])
+        load_h(2, 0)
+        load_v2(0)
+        load_v2_scales(0, nc.scalar)
+        load_h(2, 1)
+        load_kfirst("v", V1, 0, 0, 512)
+        load_h(1, 0)
+        load_h(1, 1)
+        load_kfirst("v", V1, 1, 0, 512)
+        later = [("v", V1, 0, 512), ("v", V1, 1, 512), ("u1", U1, 0, 0), ("u1", U1, 1, 0), ("u2", U2, 0, 0), ("u2", U2, 1, 0)]
+        plan = {2: [], 3: [], 4: later[0:1], 5: later[1:2], 6: later[2:3], 7: later[3:4]}
+        for i in range(2, ROW_TILES):
+            for key, src, c, col0 in plan[i]:
+                load_kfirst(key, src, c, col0, 512)
+            load_h(2, i)
+            load_h(1, i)
+        for key, src, c, col0 in later[4:6]:
+            load_kfirst(key, src, c, col0, 512)
+        load_v2(1)
+        load_v2_scales(1, nc.sync)
+        nc.sync.dma_start(out=pw[:], in_=power.partition_broadcast(P))
+
+        def prepare(pieces):
+            for n, piece in enumerate(pieces):
+                interleave(piece, "V")
+                if n > 0:
+                    quantize_piece(pieces[n - 1])
+            quantize_piece(pieces[-1])
+
+        for part in range(2):
+            turn_h(0, part)
+            quantize_h(0, part)
+        wide_passes(0, 0, 0, 3)
+        for part in range(2):
+            turn_h(1, part)
+        interleave(("v", 0, 0), "V")
+        quantize_h(1, 0)
+        quantize_piece(("v", 0, 0))
+        interleave(("v", 0, 1), "V")
+        quantize_h(1, 1)
+        quantize_piece(("v", 0, 1))
+        for i in range(2):
+            turn_h(i, 2)
+        wide_passes(1, 0, 0, 3)
+        quantize_h(0, 2)
+        interleave(("v", 1, 0), "V")
+        quantize_h(1, 2)
+        quantize_piece(("v", 1, 0))
+        interleave(("v", 1, 1), "V")
+        for i in range(2):
+            wide_passes(i, 0, 3, 4)
+        for part in range(3):
+            turn_h(2, part)
+        quantize_piece(("v", 1, 1))
+        for i in range(2):
+            wide_passes(i, 0, 4, 5)
+            empty_wide(i, 0)
+        for part in range(3):
+            quantize_h(2, part)
+
+        pending = []
+        vfill = {2: [("v", 0, 2), ("v", 0, 3)], 3: [("v", 1, 2), ("v", 1, 3)], 4: [("u1", 0, 0), ("u1", 0, 1)], 5: [("g", 0, 0), ("g", 0, 1)], 6: [("u1", 1, 0), ("u1", 1, 1)], 7: [("u2", 0, 0), ("u2", 0, 1)]}
+        sfill = {2: [], 3: [], 4: [], 5: [], 6: [("u2", 1, 0)], 7: [("u2", 1, 1)]}
+        for i in range(2, ROW_TILES):
+            mine = vfill[i]
+            if i + 1 < ROW_TILES:
+                for part in range(3):
+                    turn_h(i + 1, part)
+                    if part < len(mine):
+                        interleave(mine[part], "V")
+                    quantize_h(i + 1, part)
+                    if part < len(mine):
+                        quantize_piece(mine[part])
+            elif mine:
+                prepare(mine)
+            wide_passes(i, 0, 0, 5)
+            empty_wide(i, 0)
+            for piece in sfill[i]:
+                interleave(piece, "S")
+                pending.append(piece)
+
+        def g_unit(g, j):
+            g_bank[g, j] = next_bank()
+            for t in range(PACK):
+                g_passes(PACK * g + t, g_bank[g, j][:, t * CH : (t + 1) * CH], j * CH, CH, 0, 5)
+            empty_g(g, j)
+
+        def w_unit(i):
+            wide_passes(i, 1, 0, 5)
+            empty_wide(i, 1)
+
+        def f_unit(j0, nj):
+            for b in range(2 * nj):
+                f_passes(j0, nj, b)
+
+        def finish(j0, nj, between=()):
+            nb, per = 2 * nj, 2 // nj
+            extra = list(between)
+            for b in range(nb):
+                add_squares(j0, nj, b, per)
+                if b > 0:
+                    weigh(j0, nj, b - 1, per)
+                if extra:
+                    extra.pop(0)()
+            weigh(j0, nj, nb - 1, per)
+            for call in extra:
+                call()
+            store_y(j0, nj)
+
+        w_unit(0)
+        quantize_piece(pending[0])
+        prepare([("g", 1, 0), ("g", 1, 1)])
+        quantize_piece(pending[1])
+        w_unit(1)
+        w_unit(2)
+        f_unit(0, 2)
+        finish(0, 2)
+        w_unit(3)
+        round_y(0, 0)
+        round_y(0, 1)
+        prepare([("g", 0, 2), ("g", 0, 3)])
+        g_unit(1, 4)
+        g_unit(1, 5)
+        quantize_g(1, 4)
+        f_unit(2, 2)
+        finish(2, 2, [lambda: quantize_g(1, 5)])
+        g_unit(1, 6)
+        round_y(2, 0)
+        round_y(2, 1)
+        quantize_g(1, 6)
+        f_unit(4, 2)
+        turn_y([0, 1])
+        turn_y([2, 3])
+        finish(4, 2)
+        quantize_y(0)
+        round_y(4, 0)
+        quantize_y(1)
+        round_y(4, 1)
+        quantize_y(2)
+        f_unit(6, 1)
+        finish(6, 1, [lambda: quantize_y(3)])
+        store_codes(0, 0, 4, [nc.sync])
+        store_scales(0, [nc.sync])
+        g_unit(1, 7)
+        turn_y([4, 5])
+        quantize_g(1, 7)
+        round_y(6, 0)
+        last = [next_bank() for a in range(4)]
+        for a in range(4):
+            f_pass(last[a], 0, 7, CH, a, 0, 0)
+        quantize_y(4)
+        for a in range(4):
+            f_pass(last[a], 0, 7, CH, a, 0, 1)
+            for g in range(2):
+                f_pass(last[a], CH, 7, CH, a, 1, g)
+            square(last[a], (7, a), 2 * CH)
+        turn_y([6])
+        quantize_y(5)
+        y_bf[7] = stage.tile([P, 4 * CH], BF16, name=fresh("yb"), tag="yb", bufs=8)
+        for a in range(4):
+            add_squares(7, 1, a, 1)
+            if a > 0:
+                nc.vector.tensor_tensor(
+                    out=y_bf[7][:, (a - 1) * CH : a * CH], in0=sum_of[7, a - 1][:, 0, :], in1=pw[:, 7 * CH :], op=MULT
+                )
+        nc.vector.tensor_tensor(out=y_bf[7][:, 3 * CH :], in0=sum_of[7, 3][:, 0, :], in1=pw[:, 7 * CH :], op=MULT)
+        turn_y([7], 2)
+        quantize_y(6)
+        store_codes(1, 0, 3, [nc.sync])
+        for a in range(4):
+            weigh(7, 1, a, 1)
+        store_y(7, 1)
+        quantize_y(7)
+        store_codes(1, 3, 4, [nc.sync, nc.scalar])
+        store_scales(1, [nc.scalar, nc.sync])

@@ -21,469 +21,414 @@ P = 128
 PACK = 4
 KP = P * PACK
 BANK = 512
-CH = 128
-NCH = D // CH
-ROW_TILES = R // P
-EARLY = 4
+PAIRS = KP // 2
+HALF = D // 2
+PART = 256
+CHUNK = 128
+USER_TILES = NU // P
+V2_PASSES = T2 // KP
+PASSES = V2_PASSES + T1 // KP
 
 
 def tile_joint_precoding_interference_leakage_k6_kernel(
     tc, H1, V1, H2, V2_words, V2_scales, U1, U2, power, out_0, out_1, out_2
 ):
     nc = tc.nc
+    vector_copy, scalar_copy = nc.vector.tensor_copy, nc.scalar.copy
+
     with ExitStack() as ctx:
         keep = ctx.enter_context(tc.tile_pool(name="keep", bufs=1))
-        stage = ctx.enter_context(tc.tile_pool(name="stage", bufs=3))
+        stage = ctx.enter_context(tc.tile_pool(name="stage", bufs=1))
         psum = ctx.enter_context(tc.psum_pool(name="psum", bufs=1))
         ctx.enter_context(tc.manual_schedule())
 
-        counter = []
+        names = []
 
-        def fresh(prefix):
-            counter.append(0)
-            return "%s%d" % (prefix, len(counter))
+        def staged(tag, shape, dtype, bufs):
+            names.append(tag)
+            return stage.tile(shape, dtype, name="%s%d" % (tag, len(names)), tag=tag, bufs=bufs, align_bytes=64)
 
-        def bank(k):
-            return psum.tile([P, BANK], F32, name=fresh("ps"), tag="bank%d" % k)
+        free_banks = list(range(8))
 
-        turns = {}
-
-        def rotate(role, banks):
-            n = turns.get(role, 0)
-            turns.update({role: n + 1})
-            return bank(banks[n % len(banks)])
+        def take_bank():
+            number = free_banks.pop(0)
+            names.append("bank")
+            return psum.tile([P, BANK], F32, name="bank_use%d" % len(names), tag="bank%d" % number), number
 
         def planes(name, width):
-            codes = keep.tile([P, width], U32, name=name + "c", align_bytes=64)
-            scales = keep.tile([P, width], U8, name=name + "s", align_bytes=64)
+            codes = keep.tile([P, width], U32, name=name + "_codes", align_bytes=64)
+            scales = keep.tile([P, width], U8, name=name + "_scales", align_bytes=64)
             return codes, scales
 
-        def quantize(pair, cols, src):
-            nc.vector.quantize_mx(out=pair[0][:, cols].bitcast(FP8X4), scales=pair[1][:, cols], in_=src)
+        def quantize(operand, cols, src):
+            nc.vector.quantize_mx(out=operand[0][:, cols].bitcast(FP8X4), scales=operand[1][:, cols], in_=src)
 
-        h_rows = {1: H1.rearrange("(g m t) k -> g t m k", g=2, t=PACK), 2: H2.rearrange("(g m t) k -> g t m k", g=2, t=PACK)}
-        h_raw = {}
-
-        def load_h(which, i):
-            width = T1 if which == 1 else T2
-            raw = keep.tile([P, width], BF16, name="h%d_%d" % (which, i))
-            nc.sync.dma_start(out=raw[:], in_=h_rows[which][i // PACK, i % PACK])
-            h_raw[which, i] = raw
-
-        v2_words = {}
-
-        def load_v2(half):
-            words = keep.tile([P, 3, D], U8, name="v2w%d" % half, align_bytes=64)
-            src = V2_words.rearrange("g p n -> p g n")[:, :, half * D : (half + 1) * D]
-            nc.sync.dma_start(out=words[:].bitcast(I32), in_=src.bitcast(I32))
-            v2_words[half] = words
-
-        v2_scale = {}
-
-        def load_v2_scales(half, engine):
-            plane = keep.tile([P, 3, BANK], U8, name="v2s%d" % half, align_bytes=64)
-            nc.vector.memset(plane[:].bitcast(I32), 0)
-            rows = V2_scales.rearrange("g q n -> q g n")[:, :, half * BANK : (half + 1) * BANK]
-            for quad in range(4):
-                engine.dma_start(
-                    out=plane[32 * quad : 32 * quad + 4].bitcast(I32), in_=rows[4 * quad : 4 * quad + 4].bitcast(I32)
-                )
-            v2_scale[half] = plane
-
-        raw_of = {}
-
-        def load_kfirst(key, src, c, col0, width):
-            raw = keep.tile([P, PACK, width], BF16, name="raw%s_%d_%d" % (key, c, col0))
-            nc.sync.dma_start(
-                out=raw[:], in_=src[c * KP : (c + 1) * KP, col0 : col0 + width].rearrange("(p j) n -> p j n", j=PACK)
+        def multiply(out, stationary, moving, start, stop):
+            nc.tensor.matmul_mx(
+                out=out, lhsT=stationary[0], lhsT_scale=stationary[1], rhs=moving[0], rhs_scale=moving[1], start=start, stop=stop
             )
-            for x in range(col0, col0 + width, 256):
-                raw_of[key, c, x // 256] = raw[:, :, x - col0 : x - col0 + 256]
 
-        kq = {}
-        grouped_of = {}
+        def columns(operand, cols):
+            return operand[0][:, cols].bitcast(FP8X4), operand[1][:, cols]
 
-        def interleave(piece, engine):
-            grouped = stage.tile([P, 256 * PACK], BF16, name=fresh("grp"), tag="grp" + engine, bufs=4, align_bytes=64)
-            dst = grouped[:].rearrange("p (c i t) -> p c t i", i=4, t=PACK)
-            src = raw_of[piece].rearrange("p t (c i) -> p c t i", i=4)
-            if engine == "V":
-                nc.vector.tensor_copy(out=dst, in_=src)
-            else:
-                nc.scalar.copy(out=dst, in_=src)
-            grouped_of[piece] = grouped
-
-        def quantize_piece(piece):
-            key, c, x = piece
-            if (key, c, x // 2) not in kq:
-                kq[key, c, x // 2] = planes("kq%s_%d_%d" % piece, 512)
-            quantize(kq[key, c, x // 2], slice((x % 2) * 256, (x % 2 + 1) * 256), grouped_of[piece][:])
+        def turn_pairs(sources, dst):
+            bank, number = take_bank()
+            for slot, src in enumerate(sources):
+                nc.tensor.transpose(bank[:, slot * P : (slot + 1) * P], src, ident[:])
+            n = len(sources) // 2
+            scalar_copy(
+                out=dst.bitcast(F32).rearrange("p (c m u) -> p c m u", c=n, u=2),
+                in_=bank[:, : n * 2 * P].rearrange("p (c u m) -> p c m u", c=n, u=2),
+            )
+            free_banks.append(number)
 
         ident = keep.tile([P, P], F32, name="ident")
-        PARTS = ((2, 0, 2), (2, 2, 1), (1, 0, 2))
-        h_turned = {}
-        hq = {}
+        gains = keep.tile([P, D], BF16, name="gains")
+        h_rows, v2_words, v2_scales, k_first = {}, {}, {}, {}
 
-        def turn_h(i, part):
-            which, c0, n = PARTS[part]
-            words = h_raw[which, i][:].bitcast(F32)
-            ps = rotate("T", (3, 4, 5, 6, 7))
-            for c in range(n):
-                for u in range(2):
-                    w0 = 256 * (c0 + c)
-                    slot = 2 * c + u
-                    nc.tensor.transpose(ps[:, slot * P : (slot + 1) * P], words[:, w0 + u : w0 + 256 : 2], ident[:])
-            turned = stage.tile([P, 1024], BF16, name=fresh("ht"), tag="ht", bufs=4, align_bytes=64)
-            nc.scalar.copy(
-                out=turned[:, : n * KP].bitcast(F32).rearrange("p (c r u) -> p c r u", c=n, u=2),
-                in_=ps[:, : n * 256].rearrange("p (c u r) -> p c r u", c=n, u=2),
-            )
-            h_turned[i, part] = turned
+        def load_h(matrix, i):
+            src = (H1 if matrix == 1 else H2).rearrange("(g m t) k -> g t m k", g=2, t=PACK)[i // PACK, i % PACK]
+            h_rows[matrix, i] = keep.tile([P, src.shape[1]], BF16, name="h%d_%d" % (matrix, i))
+            nc.sync.dma_start(out=h_rows[matrix, i][:], in_=src)
 
-        def quantize_h(i, part):
-            n = PARTS[part][2]
-            hq[i, part] = planes("hq%d_%d" % (i, part), n * P)
-            quantize(hq[i, part], slice(0, n * P), h_turned[i, part][:, : n * KP])
+        def load_v2_words(half):
+            v2_words[half] = keep.tile([P, V2_PASSES, 2 * HALF], U8, name="v2_words%d" % half, align_bytes=64)
+            src = V2_words.rearrange("g p n -> p g n")[:, :, half * 2 * HALF : (half + 1) * 2 * HALF]
+            nc.sync.dma_start(out=v2_words[half][:].bitcast(I32), in_=src.bitcast(I32))
 
-        g_bank = {}
+        def clear_v2_scales(half, engine):
+            v2_scales[half] = keep.tile([P, V2_PASSES, HALF], U8, name="v2_scales%d" % half, align_bytes=64)
+            engine.memset(v2_scales[half][:].bitcast(I32), 0)
 
-        def g_passes(i, out, d0, w, first, last):
-            half, x0 = divmod(d0, BANK)
-            for c in range(first, last):
-                if c < 3:
-                    pair, off = hq[i, c // 2], (c % 2) * P
-                    rhs = v2_words[half][:, c, 2 * x0 : 2 * (x0 + w)].bitcast(FP4X4)
-                    rhs_scale = v2_scale[half][:, c, x0 : x0 + w]
-                else:
-                    pair, off = hq[i, 2], (c - 3) * P
-                    mov = kq["v", c - 3, half]
-                    rhs = mov[0][:, x0 : x0 + w].bitcast(FP8X4)
-                    rhs_scale = mov[1][:, x0 : x0 + w]
-                nc.tensor.matmul_mx(
-                    out=out,
-                    lhsT=pair[0][:, off : off + P].bitcast(FP8X4),
-                    lhsT_scale=pair[1][:, off : off + P],
-                    rhs=rhs,
-                    rhs_scale=rhs_scale,
-                    start=(c == 0),
-                    stop=(c == 4),
+        def load_v2_scales(half):
+            rows = V2_scales.rearrange("g q n -> q g n")[:, :, half * HALF : (half + 1) * HALF]
+            for quad in range(4):
+                nc.sync.dma_start(
+                    out=v2_scales[half][32 * quad : 32 * quad + 4].bitcast(I32), in_=rows[4 * quad : 4 * quad + 4].bitcast(I32)
                 )
 
+        def load_k_first(name, src, c):
+            raw = keep.tile([P, PACK, src.shape[1]], BF16, name="%s_rows%d" % (name, c))
+            nc.sync.dma_start(out=raw[:], in_=src[c * KP : (c + 1) * KP, :].rearrange("(p t) n -> p t n", t=PACK))
+            for half in range(src.shape[1] // HALF):
+                k_first[name, c, half] = raw[:, :, half * HALF : (half + 1) * HALF]
+
+        words_of, quantised = {}, {}
+        WHOLE, FIRST, SECOND = slice(0, 2 * PART), slice(0, PART), slice(PART, 2 * PART)
+
+        def interleave(key, cols, copy):
+            if key not in words_of:
+                words_of[key] = staged("words", [P, HALF * PACK], BF16, 4)
+            copy(
+                out=words_of[key][:, cols.start * PACK : cols.stop * PACK].rearrange("p (c i t) -> p c t i", i=4, t=PACK),
+                in_=k_first[key][:, :, cols].rearrange("p t (c i) -> p c t i", i=4),
+            )
+
+        def quantize_words(key, cols):
+            if key not in quantised:
+                quantised[key] = planes("%s_%d_%d" % key, HALF)
+            quantize(quantised[key], cols, words_of[key][:, cols.start * PACK : cols.stop * PACK])
+
+        blocks = [(i, c) for i in range(R // P) for c in range(PASSES)]
+        h_words, h_quantised = {}, {}
+
+        def turn_h(first, count):
+            h_words[first] = staged("h_words", [P, 4 * KP], BF16, 3)
+            for x in range(count):
+                sources = []
+                for i, c in blocks[2 * (first + x) : 2 * (first + x) + 2]:
+                    matrix, k0 = (2, c) if c < V2_PASSES else (1, c - V2_PASSES)
+                    pairs = h_rows[matrix, i][:].bitcast(F32)[:, PAIRS * k0 : PAIRS * (k0 + 1)]
+                    sources = sources + [pairs[:, 0::2], pairs[:, 1::2]]
+                turn_pairs(sources, h_words[first][:, x * 2 * KP : (x + 1) * 2 * KP])
+
+        def quantize_h(first, count):
+            operand = planes("h_bank%d" % first, 2 * count * P)
+            quantize(operand, slice(0, 2 * count * P), h_words[first][:, : count * 2 * KP])
+            for x in range(2 * count):
+                h_quantised[blocks[2 * first + x]] = columns(operand, slice(x * P, (x + 1) * P))
+
+        def g_pass(out, i, c, d0, width):
+            half, x0 = divmod(d0, HALF)
+            if c < V2_PASSES:
+                moving = v2_words[half][:, c, 2 * x0 : 2 * (x0 + width)].bitcast(FP4X4), v2_scales[half][:, c, x0 : x0 + width]
+            else:
+                moving = columns(quantised["v1", c - V2_PASSES, half], slice(x0, x0 + width))
+            multiply(out, h_quantised[i, c], moving, c == 0, c == PASSES - 1)
+
         wide_bank = {}
-        wide_bf = {}
 
         def wide_passes(i, half, first, last):
             if first == 0:
-                wide_bank[i, half] = rotate("W", (0, 1, 2)) if half == 0 else next_bank()
-            g_passes(i, wide_bank[i, half][:], half * BANK, BANK, first, last)
+                wide_bank[i, half] = take_bank()
+            for c in range(first, last):
+                g_pass(wide_bank[i, half][0][:], i, c, half * HALF, HALF)
 
-        def empty_wide(i, half):
+        def empty_wide(i, half, copy):
             g, t = divmod(i, PACK)
             if t == 0:
-                wide_bf[g, half] = stage.tile([P, PACK, BANK], BF16, name=fresh("gw"), tag="gw", bufs=2)
-                for x in range(2):
-                    raw_of["g", g, 2 * half + x] = wide_bf[g, half][:, :, 256 * x : 256 * (x + 1)]
-            nc.scalar.copy(out=wide_bf[g, half][:, t, :], in_=wide_bank[i, half][:])
+                rows = staged("g_rows", [P, PACK, HALF], BF16, 3)
+                k_first["g", g, half] = rows[:]
+            copy(out=k_first["g", g, half][:, t, :], in_=wide_bank[i, half][0][:])
+            free_banks.append(wide_bank[i, half][1])
 
-        g_bf = {}
-        gq = {}
+        def wide_blocks(first, last):
+            for i, c in blocks[first:last]:
+                wide_passes(i, 0, c, c + 1)
+                if c == PASSES - 1:
+                    empty_wide(i, 0, scalar_copy)
 
-        def empty_g(g, j, engine="S"):
-            dst = stage.tile([P, CH * PACK], BF16, name=fresh("gb"), tag="gb", bufs=5, align_bytes=64)
-            o = dst[:].rearrange("p (d t) -> p d t", t=PACK)
-            s = g_bank[g, j][:].rearrange("p (t d) -> p d t", t=PACK)
-            if engine == "V":
-                nc.vector.tensor_copy(out=o, in_=s)
-            else:
-                nc.scalar.copy(out=o, in_=s)
-            g_bf[g, j] = dst
+        g_chunk = {}
 
-        def quantize_g(g, j):
-            if j % 4 == 0:
-                kq["g", g, j // 4] = planes("gq%d_%d" % (g, j // 4), BANK)
-            quantize(kq["g", g, j // 4], slice((j % 4) * CH, (j % 4 + 1) * CH), g_bf[g, j][:])
-
-        pw = keep.tile([P, D], BF16, name="pw")
-        order = [2, 3, 4, 0, 5, 6, 7, 1]
-        taken = []
-
-        def next_bank():
-            taken.append(0)
-            return bank(order[(len(taken) - 1) % 8])
-
-        sq_of = {}
-        y_of = {}
-
-        def f_pass(ps, o, j0, w, a, f, g):
-            st = kq["u%d" % (f + 1), g, 0]
-            mov = kq["g", g, j0 // 4]
-            cols = slice((j0 % 4) * CH, (j0 % 4) * CH + w)
-            nc.tensor.matmul_mx(
-                out=ps[:, o : o + w],
-                lhsT=st[0][:, a * P : (a + 1) * P].bitcast(FP8X4),
-                lhsT_scale=st[1][:, a * P : (a + 1) * P],
-                rhs=mov[0][:, cols].bitcast(FP8X4),
-                rhs_scale=mov[1][:, cols],
-                start=(g == 0),
-                stop=(g == 1),
+        def narrow_g(j):
+            bank, number = take_bank()
+            for t in range(PACK):
+                for c in range(PASSES):
+                    g_pass(bank[:, t * CHUNK : (t + 1) * CHUNK], PACK + t, c, j * CHUNK, CHUNK)
+            g_chunk[j] = staged("g_chunk", [P, CHUNK * PACK], BF16, 2)
+            scalar_copy(
+                out=g_chunk[j][:].rearrange("p (d t) -> p d t", t=PACK), in_=bank[:].rearrange("p (t d) -> p d t", t=PACK)
             )
+            free_banks.append(number)
 
-        def square(ps, key, width):
-            sq = stage.tile([P, BANK], F32, name=fresh("sq"), tag="sq", bufs=4)
-            nc.scalar.activation(out=sq[:, :width], in_=ps[:, :width], func=SQUARE)
-            sq_of[key] = sq[:, :width]
+        quantised["g", 1, 1] = planes("g_1_1", HALF)
 
-        def f_passes(j0, nj, b):
-            w = nj * CH
-            per = 2 // nj
-            ps = next_bank()
-            for al in range(per):
-                for f in range(2):
-                    for g in range(2):
-                        f_pass(ps, (2 * al + f) * w, j0, w, b * per + al, f, g)
-            square(ps, (j0, b), BANK)
+        def quantize_narrow(j):
+            quantize(quantised["g", 1, 1], slice((j % 4) * CHUNK, (j % 4 + 1) * CHUNK), g_chunk[j][:])
 
-        sum_of = {}
+        squares, sums, y_rows, y_pairs, y_words = {}, {}, {}, {}, {}
 
-        def add_squares(j0, nj, b, per):
-            w = nj * CH
-            v = sq_of[j0, b].rearrange("p (a f w) -> p a f w", f=2, w=w)
-            s = stage.tile([P, per, w], F32, name=fresh("sum"), tag="sum", bufs=4)
-            nc.vector.tensor_tensor(out=s[:], in0=v[:, :, 0, :], in1=v[:, :, 1, :], op=ADD)
-            sum_of[j0, b] = s
+        def f_pass(out, j, width, a, f, g):
+            x0 = (j % 4) * CHUNK
+            stationary = columns(quantised["u%d" % (f + 1), g, 0], slice(a * P, (a + 1) * P))
+            multiply(out, stationary, columns(quantised["g", g, j // 4], slice(x0, x0 + width)), g == 0, g == 1)
 
-        def weigh(j0, nj, b, per):
-            w = nj * CH
-            if b == 0:
-                y_of[j0] = stage.tile([P, 4, w], F32, name=fresh("y"), tag="y", bufs=3)
-            gain = pw[:, j0 * CH : j0 * CH + w].unsqueeze(1).to_broadcast([P, per, w])
-            nc.vector.tensor_tensor(out=y_of[j0][:, b * per : (b + 1) * per, :], in0=sum_of[j0, b][:], in1=gain, op=MULT)
+        def square(held, key, place, width):
+            if place == 0:
+                squares[key] = staged("squares", [P, 2 * BANK], F32, 3)
+            nc.scalar.activation(out=squares[key][:, place * width : (place + 1) * width], in_=held[0][:, :width], func=SQUARE)
+            free_banks.append(held[1])
 
-        def store_y(j0, nj):
-            dst = out_0[:, j0 * CH : (j0 + nj) * CH].rearrange("(a u) d -> u a d", u=P)
-            nc.sync.dma_start(out=dst, in_=y_of[j0][:])
+        def f_unit(j, width):
+            per_bank = BANK // (2 * width)
+            for b in range(USER_TILES // per_bank):
+                held = take_bank()
+                for x in range(per_bank):
+                    for f in range(2):
+                        o = (2 * x + f) * width
+                        for g in range(2):
+                            f_pass(held[0][:, o : o + width], j, width, b * per_bank + x, f, g)
+                square(held, (j, b // 2), b % 2, BANK)
 
-        y_bf = {}
+        def add_filters(j, width, part, tiles):
+            both = squares[j, part][:, : tiles * 2 * width].rearrange("p (a f w) -> p a f w", f=2, w=width)
+            sums[j, part] = staged("sums", [P, tiles, width], F32, 3)
+            nc.vector.tensor_tensor(out=sums[j, part][:], in0=both[:, :, 0, :], in1=both[:, :, 1, :], op=ADD)
 
-        def round_y(j0, jj, engine="V"):
-            dst = stage.tile([P, 4 * CH], BF16, name=fresh("yb"), tag="yb", bufs=8)
-            (nc.vector.tensor_copy if engine == "V" else nc.scalar.copy)(
-                out=dst[:].rearrange("p (u a q e) -> p u a q e", u=2, a=4, e=2),
-                in_=y_of[j0][:, :, jj * CH : (jj + 1) * CH].rearrange("p a (q u e) -> p u a q e", u=2, e=2),
+        def times_power(out, j, width, part, tiles):
+            gain = gains[:, j * CHUNK : j * CHUNK + width].unsqueeze(1).to_broadcast([P, tiles, width])
+            nc.vector.tensor_tensor(out=out, in0=sums[j, part][:], in1=gain, op=MULT)
+
+        def weigh(j, width, part, tiles):
+            if part == 0:
+                y_rows[j] = staged("y_rows", [P, USER_TILES, width], F32, 3)
+            times_power(y_rows[j][:, part * tiles : (part + 1) * tiles, :], j, width, part, tiles)
+
+        def store_y(j, width, tiles=slice(0, USER_TILES)):
+            dst = out_0[:, j * CHUNK : j * CHUNK + width].rearrange("(a m) d -> m a d", m=P)
+            nc.sync.dma_start(out=dst[:, tiles, :], in_=y_rows[j][:, tiles, :])
+
+        def round_y(unit, x, copy):
+            dst = staged("y_pairs", [P, USER_TILES * CHUNK], BF16, 7)
+            copy(
+                out=dst[:].rearrange("p (u a q e) -> p u a q e", u=2, a=USER_TILES, e=2),
+                in_=y_rows[unit][:, :, x * CHUNK : (x + 1) * CHUNK].rearrange("p a (q u e) -> p u a q e", u=2, e=2),
             )
-            y_bf[j0 + jj] = dst
+            pairs = dst[:].bitcast(F32)
+            y_pairs[unit + x] = [pairs[:, :P], pairs[:, P:]]
 
-        y_turned = {}
+        def turn_y(j, count):
+            y_words[j] = staged("y_words", [P, 2 * KP], BF16, 3)
+            turn_pairs([src for x in range(count) for src in y_pairs[j + x]], y_words[j][:, : count * KP])
 
-        def turn_y(js, step=1):
-            ps = next_bank()
-            n = len(js)
-            for x, j in enumerate(js):
-                words = y_bf[j][:].bitcast(F32)
-                for u in range(2):
-                    slot = 2 * x + u
-                    nc.tensor.transpose(ps[:, slot * P : (slot + 1) * P], words[:, u * P : (u + 1) * P] if step == 1 else words[:, u::2], ident[:])
-            turned = stage.tile([P, 1024], BF16, name=fresh("yt"), tag="ht", bufs=4, align_bytes=64)
-            nc.scalar.copy(
-                out=turned[:, : n * KP].bitcast(F32).rearrange("p (c r u) -> p c r u", c=n, u=2),
-                in_=ps[:, : n * 256].rearrange("p (c u r) -> p c r u", c=n, u=2),
-            )
-            for x, j in enumerate(js):
-                y_turned[j] = turned[:, x * KP : (x + 1) * KP]
+        y_planes = [planes("y%d" % g, 4 * P) for g in range(2)]
 
-        y_codes = [keep.tile([P, 4 * P], U32, name="yc%d" % g, align_bytes=64) for g in range(2)]
-        y_scales = [keep.tile([P, P], U8, name="ys%d" % g, align_bytes=64) for g in range(2)]
+        def quantize_y(j, count):
+            quantize(y_planes[j // 4], slice((j % 4) * P, (j % 4 + count) * P), y_words[j][:, : count * KP])
 
-        def quantize_y(j):
-            g, jj = divmod(j, 4)
-            nc.vector.quantize_mx(
-                out=y_codes[g][:, jj * P : (jj + 1) * P].bitcast(FP8X4), scales=y_scales[g][4 * jj :, :], in_=y_turned[j]
-            )
+        def store_planes(g, code_queues, scale_queues):
+            codes = out_1[g].rearrange("(x q) (a m) t -> a q x (m t)", x=4, a=USER_TILES)
+            scales = out_2[g].rearrange("(x r) (a m) -> a r x m", r=4, a=USER_TILES)
+            for a in range(USER_TILES):
+                src = y_planes[g][0][32 * a : 32 * a + 32, :].rearrange("q (x m) -> q x m", m=P)
+                code_queues[a % 2].dma_start(out=codes[a].bitcast(I32), in_=src.bitcast(I32))
+            for a in range(USER_TILES):
+                src = y_planes[g][1][32 * a : 32 * a + 4, :].rearrange("r (x m) -> r x m", m=P)
+                scale_queues[a % 2].dma_start(out=scales[a].bitcast(I32), in_=src.bitcast(I32))
 
-        def store_codes(g, first, last, engines):
-            dst = out_1[g].rearrange("(j q) (a m) t -> a q j (m t)", j=4, a=4)
-            for a in range(4):
-                src = y_codes[g][32 * a : 32 * a + 32, first * P : last * P].rearrange("q (j m) -> q j m", m=P)
-                engines[a % len(engines)].dma_start(out=dst[a, :, first:last, :].bitcast(I32), in_=src.bitcast(I32))
-
-        def store_scales(g, engines):
-            for a in range(4):
-                engines[a % len(engines)].dma_start(
-                    out=out_2[g, :, a * P : (a + 1) * P].bitcast(I32), in_=y_scales[g][32 * a : 32 * a + 16, :].bitcast(I32)
-                )
-
+        clear_v2_scales(0, nc.gpsimd)
         make_identity(nc, ident[:])
-        load_h(2, 0)
-        load_v2(0)
-        load_v2_scales(0, nc.scalar)
-        load_h(2, 1)
-        load_kfirst("v", V1, 0, 0, 512)
-        load_h(1, 0)
-        load_h(1, 1)
-        load_kfirst("v", V1, 1, 0, 512)
-        later = [("v", V1, 0, 512), ("v", V1, 1, 512), ("u1", U1, 0, 0), ("u1", U1, 1, 0), ("u2", U2, 0, 0), ("u2", U2, 1, 0)]
-        plan = {2: [], 3: [], 4: later[0:1], 5: later[1:2], 6: later[2:3], 7: later[3:4]}
-        for i in range(2, ROW_TILES):
-            for key, src, c, col0 in plan[i]:
-                load_kfirst(key, src, c, col0, 512)
+        clear_v2_scales(1, nc.vector)
+
+        def load_row_tile(i):
             load_h(2, i)
             load_h(1, i)
-        for key, src, c, col0 in later[4:6]:
-            load_kfirst(key, src, c, col0, 512)
-        load_v2(1)
-        load_v2_scales(1, nc.sync)
-        nc.sync.dma_start(out=pw[:], in_=power.partition_broadcast(P))
 
-        def prepare(pieces):
-            for n, piece in enumerate(pieces):
-                interleave(piece, "V")
-                if n > 0:
-                    quantize_piece(pieces[n - 1])
-            quantize_piece(pieces[-1])
+        load_row_tile(0)
+        load_v2_scales(0)
+        load_row_tile(1)
+        load_v2_words(0)
+        load_v2_scales(1)
+        load_v2_words(1)
+        load_row_tile(2)
+        load_k_first("v1", V1, 0)
+        load_k_first("v1", V1, 1)
+        load_row_tile(3)
+        for i, (name, src, c) in zip(range(4, 8), (("u1", U1, 0), ("u1", U1, 1), ("u2", U2, 0), ("u2", U2, 1))):
+            load_row_tile(i)
+            load_k_first(name, src, c)
+        nc.sync.dma_start(out=gains[:], in_=power.partition_broadcast(P))
 
+        for first, count in ((0, 1), (1, 2), (3, 2)):
+            turn_h(first, count)
+            quantize_h(first, count)
+        for i in range(2):
+            wide_passes(i, 0, 0, V2_PASSES)
+        for b in (5, 6):
+            turn_h(b, 1)
+        for b in (5, 6):
+            quantize_h(b, 1)
+        for i, half in ((0, 1), (1, 1), (2, 0), (2, 1)):
+            wide_passes(i, half, 0, V2_PASSES)
+        interleave(("v1", 0, 0), FIRST, vector_copy)
+        interleave(("v1", 0, 0), SECOND, scalar_copy)
+        quantize_words(("v1", 0, 0), FIRST)
+        interleave(("v1", 0, 1), FIRST, vector_copy)
+        quantize_words(("v1", 0, 0), SECOND)
+        interleave(("v1", 0, 1), SECOND, scalar_copy)
+        quantize_words(("v1", 0, 1), FIRST)
+        quantize_words(("v1", 0, 1), SECOND)
+        for half in range(2):
+            for i in range(3):
+                wide_passes(i, half, V2_PASSES, V2_PASSES + 1)
+        interleave(("v1", 1, 0), WHOLE, vector_copy)
+        interleave(("v1", 1, 1), WHOLE, scalar_copy)
+        quantize_words(("v1", 1, 0), WHOLE)
+        turn_h(7, 2)
+        quantize_words(("v1", 1, 1), WHOLE)
+        for half in range(2):
+            for i in range(2):
+                wide_passes(i, half, PASSES - 1, PASSES)
+        empty_wide(0, 0, vector_copy)
+        empty_wide(1, 0, scalar_copy)
+        quantize_h(7, 2)
+        empty_wide(0, 1, vector_copy)
+
+        turn_h(9, 2)
+        empty_wide(1, 1, scalar_copy)
+        interleave(("u1", 0, 0), WHOLE, vector_copy)
+        quantize_h(9, 2)
+        quantize_words(("u1", 0, 0), WHOLE)
+        wide_blocks(14, 15)
+        wide_passes(2, 1, PASSES - 1, PASSES)
+        empty_wide(2, 1, scalar_copy)
+        wide_blocks(15, 18)
+        for first, key in ((11, ("u1", 1, 0)), (13, ("g", 0, 0))):
+            turn_h(first, 2)
+            interleave(key, WHOLE, vector_copy)
+            quantize_h(first, 2)
+            quantize_words(key, WHOLE)
+            wide_blocks(2 * first - 4, 2 * first)
+        turn_h(15, 2)
+        interleave(("u2", 0, 0), FIRST, vector_copy)
+        quantize_h(15, 2)
+        interleave(("u2", 0, 0), SECOND, vector_copy)
+        wide_blocks(26, 30)
+        turn_h(17, 2)
+        quantize_words(("u2", 0, 0), WHOLE)
+        quantize_h(17, 2)
+        wide_blocks(30, 32)
+        turn_h(19, 1)
+        interleave(("u2", 1, 0), FIRST, vector_copy)
+        quantize_h(19, 1)
+        interleave(("u2", 1, 0), SECOND, scalar_copy)
+        wide_blocks(32, 40)
+        quantize_words(("u2", 1, 0), WHOLE)
+        for cols in (FIRST, SECOND):
+            interleave(("g", 1, 0), cols, vector_copy)
+            quantize_words(("g", 1, 0), cols)
+        wide_passes(3, 1, 0, PASSES)
+        empty_wide(3, 1, scalar_copy)
+        narrow_g(4)
+
+        f_unit(0, 2 * CHUNK)
+        interleave(("g", 0, 1), WHOLE, vector_copy)
+        quantize_words(("g", 0, 1), WHOLE)
+        quantize_narrow(4)
         for part in range(2):
-            turn_h(0, part)
-            quantize_h(0, part)
-        wide_passes(0, 0, 0, 3)
+            add_filters(0, 2 * CHUNK, part, 2)
         for part in range(2):
-            turn_h(1, part)
-        interleave(("v", 0, 0), "V")
-        quantize_h(1, 0)
-        quantize_piece(("v", 0, 0))
-        interleave(("v", 0, 1), "V")
-        quantize_h(1, 1)
-        quantize_piece(("v", 0, 1))
-        for i in range(2):
-            turn_h(i, 2)
-        wide_passes(1, 0, 0, 3)
-        quantize_h(0, 2)
-        interleave(("v", 1, 0), "V")
-        quantize_h(1, 2)
-        quantize_piece(("v", 1, 0))
-        interleave(("v", 1, 1), "V")
-        for i in range(2):
-            wide_passes(i, 0, 3, 4)
-        for part in range(3):
-            turn_h(2, part)
-        quantize_piece(("v", 1, 1))
-        for i in range(2):
-            wide_passes(i, 0, 4, 5)
-            empty_wide(i, 0)
-        for part in range(3):
-            quantize_h(2, part)
+            weigh(0, 2 * CHUNK, part, 2)
+        store_y(0, 2 * CHUNK)
+        f_unit(2, 2 * CHUNK)
+        round_y(0, 0, scalar_copy)
+        round_y(0, 1, vector_copy)
+        for part in range(2):
+            add_filters(2, 2 * CHUNK, part, 2)
+        narrow_g(5)
+        quantize_narrow(5)
+        for part in range(2):
+            weigh(2, 2 * CHUNK, part, 2)
+        store_y(2, 2 * CHUNK)
+        f_unit(4, CHUNK)
+        round_y(2, 0, scalar_copy)
+        round_y(2, 1, vector_copy)
+        add_filters(4, CHUNK, 0, USER_TILES)
+        weigh(4, CHUNK, 0, USER_TILES)
+        store_y(4, CHUNK)
+        narrow_g(6)
+        round_y(4, 0, vector_copy)
+        f_unit(5, CHUNK)
+        quantize_narrow(6)
+        turn_y(0, 2)
+        turn_y(2, 2)
+        add_filters(5, CHUNK, 0, USER_TILES)
+        quantize_y(0, 2)
+        weigh(5, CHUNK, 0, USER_TILES)
+        store_y(5, CHUNK)
+        quantize_y(2, 2)
+        store_planes(0, (nc.sync, nc.sync), (nc.sync, nc.sync))
+        narrow_g(7)
+        f_unit(6, CHUNK)
+        quantize_narrow(7)
+        round_y(5, 0, vector_copy)
 
-        pending = []
-        vfill = {2: [("v", 0, 2), ("v", 0, 3)], 3: [("v", 1, 2), ("v", 1, 3)], 4: [("u1", 0, 0), ("u1", 0, 1)], 5: [("g", 0, 0), ("g", 0, 1)], 6: [("u1", 1, 0), ("u1", 1, 1)], 7: [("u2", 0, 0), ("u2", 0, 1)]}
-        sfill = {2: [], 3: [], 4: [], 5: [], 6: [("u2", 1, 0)], 7: [("u2", 1, 1)]}
-        for i in range(2, ROW_TILES):
-            mine = vfill[i]
-            if i + 1 < ROW_TILES:
-                for part in range(3):
-                    turn_h(i + 1, part)
-                    if part < len(mine):
-                        interleave(mine[part], "V")
-                    quantize_h(i + 1, part)
-                    if part < len(mine):
-                        quantize_piece(mine[part])
-            elif mine:
-                prepare(mine)
-            wide_passes(i, 0, 0, 5)
-            empty_wide(i, 0)
-            for piece in sfill[i]:
-                interleave(piece, "S")
-                pending.append(piece)
-
-        def g_unit(g, j):
-            g_bank[g, j] = next_bank()
-            for t in range(PACK):
-                g_passes(PACK * g + t, g_bank[g, j][:, t * CH : (t + 1) * CH], j * CH, CH, 0, 5)
-            empty_g(g, j)
-
-        def w_unit(i):
-            wide_passes(i, 1, 0, 5)
-            empty_wide(i, 1)
-
-        def f_unit(j0, nj):
-            for b in range(2 * nj):
-                f_passes(j0, nj, b)
-
-        def finish(j0, nj, between=()):
-            nb, per = 2 * nj, 2 // nj
-            extra = list(between)
-            for b in range(nb):
-                add_squares(j0, nj, b, per)
-                if b > 0:
-                    weigh(j0, nj, b - 1, per)
-                if extra:
-                    extra.pop(0)()
-            weigh(j0, nj, nb - 1, per)
-            for call in extra:
-                call()
-            store_y(j0, nj)
-
-        w_unit(0)
-        quantize_piece(pending[0])
-        prepare([("g", 1, 0), ("g", 1, 1)])
-        quantize_piece(pending[1])
-        w_unit(1)
-        w_unit(2)
-        f_unit(0, 2)
-        finish(0, 2)
-        w_unit(3)
-        round_y(0, 0)
-        round_y(0, 1)
-        prepare([("g", 0, 2), ("g", 0, 3)])
-        g_unit(1, 4)
-        g_unit(1, 5)
-        quantize_g(1, 4)
-        f_unit(2, 2)
-        finish(2, 2, [lambda: quantize_g(1, 5)])
-        g_unit(1, 6)
-        round_y(2, 0)
-        round_y(2, 1)
-        quantize_g(1, 6)
-        f_unit(4, 2)
-        turn_y([0, 1])
-        turn_y([2, 3])
-        finish(4, 2)
-        quantize_y(0)
-        round_y(4, 0)
-        quantize_y(1)
-        round_y(4, 1)
-        quantize_y(2)
-        f_unit(6, 1)
-        finish(6, 1, [lambda: quantize_y(3)])
-        store_codes(0, 0, 4, [nc.sync])
-        store_scales(0, [nc.sync])
-        g_unit(1, 7)
-        turn_y([4, 5])
-        quantize_g(1, 7)
-        round_y(6, 0)
-        last = [next_bank() for a in range(4)]
-        for a in range(4):
-            f_pass(last[a], 0, 7, CH, a, 0, 0)
-        quantize_y(4)
-        for a in range(4):
-            f_pass(last[a], 0, 7, CH, a, 0, 1)
+        last = [take_bank() for a in range(USER_TILES)]
+        for a in range(USER_TILES):
+            f_pass(last[a][0][:, :CHUNK], 7, CHUNK, a, 0, 0)
+        for a in range(USER_TILES):
+            f_pass(last[a][0][:, :CHUNK], 7, CHUNK, a, 0, 1)
             for g in range(2):
-                f_pass(last[a], CH, 7, CH, a, 1, g)
-            square(last[a], (7, a), 2 * CH)
-        turn_y([6])
-        quantize_y(5)
-        y_bf[7] = stage.tile([P, 4 * CH], BF16, name=fresh("yb"), tag="yb", bufs=8)
-        for a in range(4):
-            add_squares(7, 1, a, 1)
-            if a > 0:
-                nc.vector.tensor_tensor(
-                    out=y_bf[7][:, (a - 1) * CH : a * CH], in0=sum_of[7, a - 1][:, 0, :], in1=pw[:, 7 * CH :], op=MULT
-                )
-        nc.vector.tensor_tensor(out=y_bf[7][:, 3 * CH :], in0=sum_of[7, 3][:, 0, :], in1=pw[:, 7 * CH :], op=MULT)
-        turn_y([7], 2)
-        quantize_y(6)
-        store_codes(1, 0, 3, [nc.sync])
-        for a in range(4):
-            weigh(7, 1, a, 1)
-        store_y(7, 1)
-        quantize_y(7)
-        store_codes(1, 3, 4, [nc.sync, nc.scalar])
-        store_scales(1, [nc.scalar, nc.sync])
+                f_pass(last[a][0][:, CHUNK : 2 * CHUNK], 7, CHUNK, a, 1, g)
+            square(last[a], (7, a // 2), a % 2, 2 * CHUNK)
+        add_filters(6, CHUNK, 0, USER_TILES)
+        add_filters(7, CHUNK, 0, 2)
+        weigh(6, CHUNK, 0, USER_TILES)
+        store_y(6, CHUNK)
+        round_y(6, 0, scalar_copy)
+        turn_y(4, 2)
+        turn_y(6, 1)
+        add_filters(7, CHUNK, 1, 2)
+        weigh(7, CHUNK, 0, 2)
+        store_y(7, CHUNK, slice(0, 2))
+        rounded = staged("y_pairs", [P, USER_TILES * CHUNK], BF16, 7)
+        times_power(rounded[:, 2 * CHUNK :].rearrange("p (a d) -> p a d", a=2), 7, CHUNK, 1, 2)
+        vector_copy(out=rounded[:, : 2 * CHUNK], in_=y_rows[7][:, :2, :].rearrange("p a d -> p (a d)"))
+        y_pairs[7] = [rounded[:].bitcast(F32)[:, 0::2], rounded[:].bitcast(F32)[:, 1::2]]
+        turn_y(7, 1)
+        weigh(7, CHUNK, 1, 2)
+        store_y(7, CHUNK, slice(2, 4))
+        quantize_y(4, 2)
+        quantize_y(6, 1)
+        quantize_y(7, 1)
+        store_planes(1, (nc.sync, nc.scalar), (nc.scalar, nc.sync))

@@ -130,17 +130,28 @@ def tile_joint_precoding_interference_leakage_k6_kernel(
             quantize(quantised[key], cols, words_of[key][:, cols.start * PACK : cols.stop * PACK])
 
         blocks = [(i, c) for i in range(R // P) for c in range(PASSES)]
-        h_words, h_quantised = {}, {}
+        h_sorted, h_words, h_quantised = {}, {}, {}
+
+        def h_pairs(i, c):
+            matrix, k0 = (2, c) if c < V2_PASSES else (1, c - V2_PASSES)
+            return h_rows[matrix, i][:].bitcast(F32)[:, PAIRS * k0 : PAIRS * (k0 + 1)]
+
+        def sort_h(b):
+            h_sorted[b] = staged("h_sorted", [P, 2 * PAIRS], F32, 3)
+            for x in range(2):
+                vector_copy(
+                    out=h_sorted[b][:, PAIRS * x : PAIRS * (x + 1)].rearrange("p (u q i) -> p q u i", u=2, i=4),
+                    in_=h_pairs(*blocks[2 * b + x]).rearrange("p (q i u) -> p q u i", u=2, i=4),
+                )
 
         def turn_h(first, count):
             h_words[first] = staged("h_words", [P, 4 * KP], BF16, 3)
-            for x in range(count):
-                sources = []
-                for i, c in blocks[2 * (first + x) : 2 * (first + x) + 2]:
-                    matrix, k0 = (2, c) if c < V2_PASSES else (1, c - V2_PASSES)
-                    pairs = h_rows[matrix, i][:].bitcast(F32)[:, PAIRS * k0 : PAIRS * (k0 + 1)]
-                    sources = sources + [pairs[:, 0::2], pairs[:, 1::2]]
-                turn_pairs(sources, h_words[first][:, x * 2 * KP : (x + 1) * 2 * KP])
+            for b in range(first, first + count):
+                if b in h_sorted:
+                    sources = [h_sorted[b][:, slot * P : (slot + 1) * P] for slot in range(4)]
+                else:
+                    sources = [h_pairs(i, c)[:, u::2] for i, c in blocks[2 * b : 2 * b + 2] for u in range(2)]
+                turn_pairs(sources, h_words[first][:, (b - first) * 2 * KP : (b - first + 1) * 2 * KP])
 
         def quantize_h(first, count):
             operand = planes("h_bank%d" % first, 2 * count * P)
@@ -283,10 +294,14 @@ def tile_joint_precoding_interference_leakage_k6_kernel(
         load_row_tile(2)
         load_k_first("v1", V1, 0)
         load_k_first("v1", V1, 1)
-        load_row_tile(3)
-        for i, (name, src, c) in zip(range(4, 8), (("u1", U1, 0), ("u1", U1, 1), ("u2", U2, 0), ("u2", U2, 1))):
+        for i in (3, 4, 5):
             load_row_tile(i)
-            load_k_first(name, src, c)
+        load_k_first("u1", U1, 0)
+        for i in (6, 7):
+            load_row_tile(i)
+        load_k_first("u1", U1, 1)
+        load_k_first("u2", U2, 0)
+        load_k_first("u2", U2, 1)
         nc.sync.dma_start(out=gains[:], in_=power.partition_broadcast(P))
 
         for first, count in ((0, 1), (1, 2), (3, 2)):
@@ -319,46 +334,62 @@ def tile_joint_precoding_interference_leakage_k6_kernel(
         for half in range(2):
             for i in range(2):
                 wide_passes(i, half, PASSES - 1, PASSES)
+        sort_h(10)
         empty_wide(0, 0, vector_copy)
+        sort_h(11)
         empty_wide(1, 0, scalar_copy)
         quantize_h(7, 2)
-        empty_wide(0, 1, vector_copy)
 
-        turn_h(9, 2)
+        def turn_run(first):
+            turn_h(first, 2)
+            turn_h(first + 2, 1)
+
+        def quantize_run(first):
+            quantize_h(first, 2)
+            quantize_h(first + 2, 1)
+
+        turn_run(9)
+        sort_h(13)
+        empty_wide(0, 1, vector_copy)
+        sort_h(14)
         empty_wide(1, 1, scalar_copy)
-        interleave(("u1", 0, 0), WHOLE, vector_copy)
-        quantize_h(9, 2)
-        quantize_words(("u1", 0, 0), WHOLE)
+        quantize_run(9)
         wide_blocks(14, 15)
         wide_passes(2, 1, PASSES - 1, PASSES)
         empty_wide(2, 1, scalar_copy)
         wide_blocks(15, 18)
-        for first, key in ((11, ("u1", 1, 0)), (13, ("g", 0, 0))):
-            turn_h(first, 2)
-            interleave(key, WHOLE, vector_copy)
-            quantize_h(first, 2)
-            quantize_words(key, WHOLE)
-            wide_blocks(2 * first - 4, 2 * first)
-        turn_h(15, 2)
+        turn_run(12)
+        interleave(("u1", 0, 0), WHOLE, vector_copy)
+        sort_h(16)
+        sort_h(17)
+        quantize_words(("u1", 0, 0), WHOLE)
+        quantize_run(12)
+        wide_blocks(18, 24)
+        turn_run(15)
+        interleave(("g", 0, 0), WHOLE, vector_copy)
+        quantize_words(("g", 0, 0), WHOLE)
+        quantize_run(15)
+        wide_blocks(24, 30)
+        for b in (18, 19):
+            turn_h(b, 1)
+        interleave(("u1", 1, 0), WHOLE, vector_copy)
+        for b in (18, 19):
+            quantize_h(b, 1)
+        interleave(("u2", 0, 0), SECOND, scalar_copy)
+        quantize_words(("u1", 1, 0), WHOLE)
+        wide_blocks(30, 35)
         interleave(("u2", 0, 0), FIRST, vector_copy)
-        quantize_h(15, 2)
-        interleave(("u2", 0, 0), SECOND, vector_copy)
-        wide_blocks(26, 30)
-        turn_h(17, 2)
         quantize_words(("u2", 0, 0), WHOLE)
-        quantize_h(17, 2)
-        wide_blocks(30, 32)
-        turn_h(19, 1)
+        wide_blocks(35, 40)
         interleave(("u2", 1, 0), FIRST, vector_copy)
-        quantize_h(19, 1)
         interleave(("u2", 1, 0), SECOND, scalar_copy)
-        wide_blocks(32, 40)
+        interleave(("g", 1, 0), FIRST, vector_copy)
+        quantize_words(("g", 1, 0), FIRST)
         quantize_words(("u2", 1, 0), WHOLE)
-        for cols in (FIRST, SECOND):
-            interleave(("g", 1, 0), cols, vector_copy)
-            quantize_words(("g", 1, 0), cols)
         wide_passes(3, 1, 0, PASSES)
         empty_wide(3, 1, scalar_copy)
+        interleave(("g", 1, 0), SECOND, vector_copy)
+        quantize_words(("g", 1, 0), SECOND)
         narrow_g(4)
 
         f_unit(0, 2 * CHUNK)

from contextlib import ExitStack

import concourse.mybir as mybir
from concourse.masks import make_identity

R, T1, T2, NU, D = 1024, 1024, 1536, 512, 1024
FLOPS = 2 * R * (T1 + T2) * D + 2 * 2 * NU * R * D

F32 = mybir.dt.float32
BF16 = mybir.dt.bfloat16
I32 = mybir.dt.int32
U32 = mybir.dt.uint32
U8 = mybir.dt.uint8
FP8X4 = mybir.dt.float8_e4m3fn_x4
FP4X4 = mybir.dt.float4_e2m1fn_x4
ADD = mybir.AluOpType.add
MULT = mybir.AluOpType.mult
SQUARE = mybir.ActivationFunctionType.Square

P = 128
PACK = 4
KP = P * PACK
BANK = 512
PAIRS = KP // 2
HALF = D // 2
PART = 256
CHUNK = 128
USER_TILES = NU // P
V2_PASSES = T2 // KP
PASSES = V2_PASSES + T1 // KP


def tile_joint_precoding_interference_leakage_k6_kernel(
    tc, H1, V1, H2, V2_words, V2_scales, U1, U2, power, out_0, out_1, out_2
):
    nc = tc.nc
    vector_copy, scalar_copy = nc.vector.tensor_copy, nc.scalar.copy

    with ExitStack() as ctx:
        keep = ctx.enter_context(tc.tile_pool(name="keep", bufs=1))
        stage = ctx.enter_context(tc.tile_pool(name="stage", bufs=1))
        psum = ctx.enter_context(tc.psum_pool(name="psum", bufs=1))
        ctx.enter_context(tc.manual_schedule())

        names = []

        def staged(tag, shape, dtype, bufs):
            names.append(tag)
            return stage.tile(shape, dtype, name="%s%d" % (tag, len(names)), tag=tag, bufs=bufs, align_bytes=64)

        free_banks = list(range(8))

        def take_bank():
            number = free_banks.pop(0)
            names.append("bank")
            return psum.tile([P, BANK], F32, name="bank_use%d" % len(names), tag="bank%d" % number), number

        def planes(name, width):
            codes = keep.tile([P, width], U32, name=name + "_codes", align_bytes=64)
            scales = keep.tile([P, width], U8, name=name + "_scales", align_bytes=64)
            return codes, scales

        def quantize(operand, cols, src):
            nc.vector.quantize_mx(out=operand[0][:, cols].bitcast(FP8X4), scales=operand[1][:, cols], in_=src)

        def multiply(out, stationary, moving, start, stop):
            nc.tensor.matmul_mx(
                out=out, lhsT=stationary[0], lhsT_scale=stationary[1], rhs=moving[0], rhs_scale=moving[1], start=start, stop=stop
            )

        def columns(operand, cols):
            return operand[0][:, cols].bitcast(FP8X4), operand[1][:, cols]

        def turn_pairs(sources, dst):
            bank, number = take_bank()
            for slot, src in enumerate(sources):
                nc.tensor.transpose(bank[:, slot * P : (slot + 1) * P], src, ident[:])
            n = len(sources) // 2
            scalar_copy(
                out=dst.bitcast(F32).rearrange("p (c m u) -> p c m u", c=n, u=2),
                in_=bank[:, : n * 2 * P].rearrange("p (c u m) -> p c m u", c=n, u=2),
            )
            free_banks.append(number)

        ident = keep.tile([P, P], F32, name="ident")
        gains = keep.tile([P, D], BF16, name="gains")
        h_rows, v2_words, v2_scales, k_first = {}, {}, {}, {}

        def load_h(matrix, i):
            src = (H1 if matrix == 1 else H2).rearrange("(g m t) k -> g t m k", g=2, t=PACK)[i // PACK, i % PACK]
            h_rows[matrix, i] = keep.tile([P, src.shape[1]], BF16, name="h%d_%d" % (matrix, i))
            nc.sync.dma_start(out=h_rows[matrix, i][:], in_=src)

        def load_v2_words(half):
            v2_words[half] = keep.tile([P, V2_PASSES, 2 * HALF], U8, name="v2_words%d" % half, align_bytes=64)
            src = V2_words.rearrange("g p n -> p g n")[:, :, half * 2 * HALF : (half + 1) * 2 * HALF]
            nc.sync.dma_start(out=v2_words[half][:].bitcast(I32), in_=src.bitcast(I32))

        def clear_v2_scales(half, engine):
            v2_scales[half] = keep.tile([P, V2_PASSES, HALF], U8, name="v2_scales%d" % half, align_bytes=64)
            engine.memset(v2_scales[half][:].bitcast(I32), 0)

        def load_v2_scales(half):
            rows = V2_scales.rearrange("g q n -> q g n")[:, :, half * HALF : (half + 1) * HALF]
            for quad in range(4):
                nc.sync.dma_start(
                    out=v2_scales[half][32 * quad : 32 * quad + 4].bitcast(I32), in_=rows[4 * quad : 4 * quad + 4].bitcast(I32)
                )

        def load_k_first(name, src, c):
            raw = keep.tile([P, PACK, src.shape[1]], BF16, name="%s_rows%d" % (name, c))
            nc.sync.dma_start(out=raw[:], in_=src[c * KP : (c + 1) * KP, :].rearrange("(p t) n -> p t n", t=PACK))
            for half in range(src.shape[1] // HALF):
                k_first[name, c, half] = raw[:, :, half * HALF : (half + 1) * HALF]

        words_of, quantised = {}, {}
        WHOLE, FIRST, SECOND = slice(0, 2 * PART), slice(0, PART), slice(PART, 2 * PART)

        def interleave(key, cols, copy):
            if key not in words_of:
                words_of[key] = staged("words", [P, HALF * PACK], BF16, 4)
            copy(
                out=words_of[key][:, cols.start * PACK : cols.stop * PACK].rearrange("p (c i t) -> p c t i", i=4, t=PACK),
                in_=k_first[key][:, :, cols].rearrange("p t (c i) -> p c t i", i=4),
            )

        def quantize_words(key, cols):
            if key not in quantised:
                quantised[key] = planes("%s_%d_%d" % key, HALF)
            quantize(quantised[key], cols, words_of[key][:, cols.start * PACK : cols.stop * PACK])

        blocks = [(i, c) for i in range(R // P) for c in range(PASSES)]
        h_sorted, h_words, h_quantised = {}, {}, {}

        def h_pairs(i, c):
            matrix, k0 = (2, c) if c < V2_PASSES else (1, c - V2_PASSES)
            return h_rows[matrix, i][:].bitcast(F32)[:, PAIRS * k0 : PAIRS * (k0 + 1)]

        def sort_h(b):
            h_sorted[b] = staged("h_sorted", [P, 2 * PAIRS], F32, 3)
            for x in range(2):
                vector_copy(
                    out=h_sorted[b][:, PAIRS * x : PAIRS * (x + 1)].rearrange("p (u q i) -> p q u i", u=2, i=4),
                    in_=h_pairs(*blocks[2 * b + x]).rearrange("p (q i u) -> p q u i", u=2, i=4),
                )

        def turn_h(first, count):
            h_words[first] = staged("h_words", [P, 4 * KP], BF16, 3)
            for b in range(first, first + count):
                if b in h_sorted:
                    sources = [h_sorted[b][:, slot * P : (slot + 1) * P] for slot in range(4)]
                else:
                    sources = [h_pairs(i, c)[:, u::2] for i, c in blocks[2 * b : 2 * b + 2] for u in range(2)]
                turn_pairs(sources, h_words[first][:, (b - first) * 2 * KP : (b - first + 1) * 2 * KP])

        def quantize_h(first, count):
            operand = planes("h_bank%d" % first, 2 * count * P)
            quantize(operand, slice(0, 2 * count * P), h_words[first][:, : count * 2 * KP])
            for x in range(2 * count):
                h_quantised[blocks[2 * first + x]] = columns(operand, slice(x * P, (x + 1) * P))

        def g_pass(out, i, c, d0, width):
            half, x0 = divmod(d0, HALF)
            if c < V2_PASSES:
                moving = v2_words[half][:, c, 2 * x0 : 2 * (x0 + width)].bitcast(FP4X4), v2_scales[half][:, c, x0 : x0 + width]
            else:
                moving = columns(quantised["v1", c - V2_PASSES, half], slice(x0, x0 + width))
            multiply(out, h_quantised[i, c], moving, c == 0, c == PASSES - 1)

        wide_bank = {}

        def wide_passes(i, half, first, last):
            if first == 0:
                wide_bank[i, half] = take_bank()
            for c in range(first, last):
                g_pass(wide_bank[i, half][0][:], i, c, half * HALF, HALF)

        def empty_wide(i, half, copy):
            g, t = divmod(i, PACK)
            if t == 0:
                rows = staged("g_rows", [P, PACK, HALF], BF16, 3)
                k_first["g", g, half] = rows[:]
            copy(out=k_first["g", g, half][:, t, :], in_=wide_bank[i, half][0][:])
            free_banks.append(wide_bank[i, half][1])

        def wide_blocks(first, last):
            for i, c in blocks[first:last]:
                wide_passes(i, 0, c, c + 1)
                if c == PASSES - 1:
                    empty_wide(i, 0, scalar_copy)

        g_chunk = {}

        def narrow_g(j):
            bank, number = take_bank()
            for t in range(PACK):
                for c in range(PASSES):
                    g_pass(bank[:, t * CHUNK : (t + 1) * CHUNK], PACK + t, c, j * CHUNK, CHUNK)
            g_chunk[j] = staged("g_chunk", [P, CHUNK * PACK], BF16, 2)
            scalar_copy(
                out=g_chunk[j][:].rearrange("p (d t) -> p d t", t=PACK), in_=bank[:].rearrange("p (t d) -> p d t", t=PACK)
            )
            free_banks.append(number)

        quantised["g", 1, 1] = planes("g_1_1", HALF)

        def quantize_narrow(j):
            quantize(quantised["g", 1, 1], slice((j % 4) * CHUNK, (j % 4 + 1) * CHUNK), g_chunk[j][:])

        squares, sums, y_rows, y_pairs, y_words = {}, {}, {}, {}, {}

        def f_pass(out, j, width, a, f, g):
            x0 = (j % 4) * CHUNK
            stationary = columns(quantised["u%d" % (f + 1), g, 0], slice(a * P, (a + 1) * P))
            multiply(out, stationary, columns(quantised["g", g, j // 4], slice(x0, x0 + width)), g == 0, g == 1)

        def square(held, key, place, width):
            if place == 0:
                squares[key] = staged("squares", [P, 2 * BANK], F32, 3)
            nc.scalar.activation(out=squares[key][:, place * width : (place + 1) * width], in_=held[0][:, :width], func=SQUARE)
            free_banks.append(held[1])

        def f_unit(j, width):
            per_bank = BANK // (2 * width)
            for b in range(USER_TILES // per_bank):
                held = take_bank()
                for x in range(per_bank):
                    for f in range(2):
                        o = (2 * x + f) * width
                        for g in range(2):
                            f_pass(held[0][:, o : o + width], j, width, b * per_bank + x, f, g)
                square(held, (j, b // 2), b % 2, BANK)

        def add_filters(j, width, part, tiles):
            both = squares[j, part][:, : tiles * 2 * width].rearrange("p (a f w) -> p a f w", f=2, w=width)
            sums[j, part] = staged("sums", [P, tiles, width], F32, 3)
            nc.vector.tensor_tensor(out=sums[j, part][:], in0=both[:, :, 0, :], in1=both[:, :, 1, :], op=ADD)

        def times_power(out, j, width, part, tiles):
            gain = gains[:, j * CHUNK : j * CHUNK + width].unsqueeze(1).to_broadcast([P, tiles, width])
            nc.vector.tensor_tensor(out=out, in0=sums[j, part][:], in1=gain, op=MULT)

        def weigh(j, width, part, tiles):
            if part == 0:
                y_rows[j] = staged("y_rows", [P, USER_TILES, width], F32, 3)
            times_power(y_rows[j][:, part * tiles : (part + 1) * tiles, :], j, width, part, tiles)

        def store_y(j, width, tiles=slice(0, USER_TILES)):
            dst = out_0[:, j * CHUNK : j * CHUNK + width].rearrange("(a m) d -> m a d", m=P)
            nc.sync.dma_start(out=dst[:, tiles, :], in_=y_rows[j][:, tiles, :])

        def round_y(unit, x, copy):
            dst = staged("y_pairs", [P, USER_TILES * CHUNK], BF16, 7)
            copy(
                out=dst[:].rearrange("p (u a q e) -> p u a q e", u=2, a=USER_TILES, e=2),
                in_=y_rows[unit][:, :, x * CHUNK : (x + 1) * CHUNK].rearrange("p a (q u e) -> p u a q e", u=2, e=2),
            )
            pairs = dst[:].bitcast(F32)
            y_pairs[unit + x] = [pairs[:, :P], pairs[:, P:]]

        def turn_y(j, count):
            y_words[j] = staged("y_words", [P, 2 * KP], BF16, 3)
            turn_pairs([src for x in range(count) for src in y_pairs[j + x]], y_words[j][:, : count * KP])

        y_planes = [planes("y%d" % g, 4 * P) for g in range(2)]

        def quantize_y(j, count):
            quantize(y_planes[j // 4], slice((j % 4) * P, (j % 4 + count) * P), y_words[j][:, : count * KP])

        def store_planes(g, code_queues, scale_queues):
            codes = out_1[g].rearrange("(x q) (a m) t -> a q x (m t)", x=4, a=USER_TILES)
            scales = out_2[g].rearrange("(x r) (a m) -> a r x m", r=4, a=USER_TILES)
            for a in range(USER_TILES):
                src = y_planes[g][0][32 * a : 32 * a + 32, :].rearrange("q (x m) -> q x m", m=P)
                code_queues[a % 2].dma_start(out=codes[a].bitcast(I32), in_=src.bitcast(I32))
            for a in range(USER_TILES):
                src = y_planes[g][1][32 * a : 32 * a + 4, :].rearrange("r (x m) -> r x m", m=P)
                scale_queues[a % 2].dma_start(out=scales[a].bitcast(I32), in_=src.bitcast(I32))

        clear_v2_scales(0, nc.gpsimd)
        make_identity(nc, ident[:])
        clear_v2_scales(1, nc.vector)

        def load_row_tile(i):
            load_h(2, i)
            load_h(1, i)

        load_row_tile(0)
        load_v2_scales(0)
        load_row_tile(1)
        load_v2_words(0)
        load_v2_scales(1)
        load_v2_words(1)
        load_row_tile(2)
        load_k_first("v1", V1, 0)
        load_k_first("v1", V1, 1)
        for i in (3, 4, 5):
            load_row_tile(i)
        load_k_first("u1", U1, 0)
        for i in (6, 7):
            load_row_tile(i)
        load_k_first("u1", U1, 1)
        load_k_first("u2", U2, 0)
        load_k_first("u2", U2, 1)
        nc.sync.dma_start(out=gains[:], in_=power.partition_broadcast(P))

        for first, count in ((0, 1), (1, 2), (3, 2)):
            turn_h(first, count)
            quantize_h(first, count)
        for i in range(2):
            wide_passes(i, 0, 0, V2_PASSES)
        for b in (5, 6):
            turn_h(b, 1)
        for b in (5, 6):
            quantize_h(b, 1)
        for i, half in ((0, 1), (1, 1), (2, 0), (2, 1)):
            wide_passes(i, half, 0, V2_PASSES)
        interleave(("v1", 0, 0), FIRST, vector_copy)
        interleave(("v1", 0, 0), SECOND, scalar_copy)
        quantize_words(("v1", 0, 0), FIRST)
        interleave(("v1", 0, 1), FIRST, vector_copy)
        quantize_words(("v1", 0, 0), SECOND)
        interleave(("v1", 0, 1), SECOND, scalar_copy)
        quantize_words(("v1", 0, 1), FIRST)
        quantize_words(("v1", 0, 1), SECOND)
        for half in range(2):
            for i in range(3):
                wide_passes(i, half, V2_PASSES, V2_PASSES + 1)
        interleave(("v1", 1, 0), WHOLE, vector_copy)
        interleave(("v1", 1, 1), WHOLE, scalar_copy)
        quantize_words(("v1", 1, 0), WHOLE)
        turn_h(7, 2)
        quantize_words(("v1", 1, 1), WHOLE)
        for half in range(2):
            for i in range(2):
                wide_passes(i, half, PASSES - 1, PASSES)
        sort_h(10)
        empty_wide(0, 0, vector_copy)
        sort_h(11)
        empty_wide(1, 0, scalar_copy)
        quantize_h(7, 2)

        def turn_run(first):
            turn_h(first, 2)
            turn_h(first + 2, 1)

        def quantize_run(first):
            quantize_h(first, 2)
            quantize_h(first + 2, 1)

        turn_run(9)
        sort_h(13)
        empty_wide(0, 1, vector_copy)
        sort_h(14)
        empty_wide(1, 1, scalar_copy)
        quantize_run(9)
        wide_blocks(14, 15)
        wide_passes(2, 1, PASSES - 1, PASSES)
        empty_wide(2, 1, scalar_copy)
        wide_blocks(15, 18)
        turn_run(12)
        interleave(("u1", 0, 0), WHOLE, vector_copy)
        sort_h(16)
        sort_h(17)
        quantize_words(("u1", 0, 0), WHOLE)
        quantize_run(12)
        wide_blocks(18, 24)
        turn_run(15)
        interleave(("g", 0, 0), WHOLE, vector_copy)
        quantize_words(("g", 0, 0), WHOLE)
        quantize_run(15)
        wide_blocks(24, 30)
        for b in (18, 19):
            turn_h(b, 1)
        interleave(("u1", 1, 0), WHOLE, vector_copy)
        for b in (18, 19):
            quantize_h(b, 1)
        interleave(("u2", 0, 0), SECOND, scalar_copy)
        quantize_words(("u1", 1, 0), WHOLE)
        wide_blocks(30, 35)
        interleave(("u2", 0, 0), FIRST, vector_copy)
        quantize_words(("u2", 0, 0), WHOLE)
        wide_blocks(35, 40)
        interleave(("u2", 1, 0), FIRST, vector_copy)
        interleave(("u2", 1, 0), SECOND, scalar_copy)
        interleave(("g", 1, 0), FIRST, vector_copy)
        quantize_words(("g", 1, 0), FIRST)
        quantize_words(("u2", 1, 0), WHOLE)
        wide_passes(3, 1, 0, PASSES)
        empty_wide(3, 1, scalar_copy)
        interleave(("g", 1, 0), SECOND, vector_copy)
        quantize_words(("g", 1, 0), SECOND)
        narrow_g(4)

        f_unit(0, 2 * CHUNK)
        interleave(("g", 0, 1), WHOLE, vector_copy)
        quantize_words(("g", 0, 1), WHOLE)
        quantize_narrow(4)
        for part in range(2):
            add_filters(0, 2 * CHUNK, part, 2)
        for part in range(2):
            weigh(0, 2 * CHUNK, part, 2)
        store_y(0, 2 * CHUNK)
        f_unit(2, 2 * CHUNK)
        round_y(0, 0, scalar_copy)
        round_y(0, 1, vector_copy)
        for part in range(2):
            add_filters(2, 2 * CHUNK, part, 2)
        narrow_g(5)
        quantize_narrow(5)
        for part in range(2):
            weigh(2, 2 * CHUNK, part, 2)
        store_y(2, 2 * CHUNK)
        f_unit(4, CHUNK)
        round_y(2, 0, scalar_copy)
        round_y(2, 1, vector_copy)
        add_filters(4, CHUNK, 0, USER_TILES)
        weigh(4, CHUNK, 0, USER_TILES)
        store_y(4, CHUNK)
        narrow_g(6)
        round_y(4, 0, vector_copy)
        f_unit(5, CHUNK)
        quantize_narrow(6)
        turn_y(0, 2)
        turn_y(2, 2)
        add_filters(5, CHUNK, 0, USER_TILES)
        quantize_y(0, 2)
        weigh(5, CHUNK, 0, USER_TILES)
        store_y(5, CHUNK)
        quantize_y(2, 2)
        store_planes(0, (nc.sync, nc.sync), (nc.sync, nc.sync))
        narrow_g(7)
        f_unit(6, CHUNK)
        quantize_narrow(7)
        round_y(5, 0, vector_copy)

        last = [take_bank() for a in range(USER_TILES)]
        for a in range(USER_TILES):
            f_pass(last[a][0][:, :CHUNK], 7, CHUNK, a, 0, 0)
        for a in range(USER_TILES):
            f_pass(last[a][0][:, :CHUNK], 7, CHUNK, a, 0, 1)
            for g in range(2):
                f_pass(last[a][0][:, CHUNK : 2 * CHUNK], 7, CHUNK, a, 1, g)
            square(last[a], (7, a // 2), a % 2, 2 * CHUNK)
        add_filters(6, CHUNK, 0, USER_TILES)
        add_filters(7, CHUNK, 0, 2)
        weigh(6, CHUNK, 0, USER_TILES)
        store_y(6, CHUNK)
        round_y(6, 0, scalar_copy)
        turn_y(4, 2)
        turn_y(6, 1)
        add_filters(7, CHUNK, 1, 2)
        weigh(7, CHUNK, 0, 2)
        store_y(7, CHUNK, slice(0, 2))
        rounded = staged("y_pairs", [P, USER_TILES * CHUNK], BF16, 7)
        times_power(rounded[:, 2 * CHUNK :].rearrange("p (a d) -> p a d", a=2), 7, CHUNK, 1, 2)
        vector_copy(out=rounded[:, : 2 * CHUNK], in_=y_rows[7][:, :2, :].rearrange("p a d -> p (a d)"))
        y_pairs[7] = [rounded[:].bitcast(F32)[:, 0::2], rounded[:].bitcast(F32)[:, 1::2]]
        turn_y(7, 1)
        weigh(7, CHUNK, 1, 2)
        store_y(7, CHUNK, slice(2, 4))
        quantize_y(4, 2)
        quantize_y(6, 1)
        quantize_y(7, 1)
        store_planes(1, (nc.sync, nc.scalar), (nc.scalar, nc.sync))
